import numpy as np
import ml_dtypes


def mxq(x, axis, fmt="e4m3"):
    dtype, down = {"e4m3": (ml_dtypes.float8_e4m3fn, 7), "e5m2": (ml_dtypes.float8_e5m2, 14)}[fmt]
    v = np.moveaxis(np.asarray(x, np.float32).astype(ml_dtypes.bfloat16).astype(np.float64), axis, -1)
    blocks = v.reshape(v.shape[:-1] + (-1, 32))
    amax = np.abs(blocks).max(-1, keepdims=True)
    byte = np.maximum(np.where(amax > 0, np.frexp(amax)[1] - 1 + 127, 0) - down, 1)
    scale = np.exp2(byte - 127.0)
    codes = (blocks / scale).astype(np.float32).astype(dtype).astype(np.float64)
    return np.moveaxis((codes * scale).reshape(v.shape), -1, axis)


WIDE = False


def mx_kscale(k):
    if not WIDE:
        return np.ones(k)
    levels = np.array([10, -10, 5, -5, 0])
    if k % 512:
        return np.exp2(np.random.permutation(np.resize(levels, k // 32))).repeat(32)
    a = np.empty((k // 512, 16))
    for p in range(k // 512):
        a[p, :8] = np.random.permutation(np.resize(levels, 8))
        for g in range(8):
            far = levels[np.abs(levels - a[p, g]) >= 10]
            a[p, g + 8] = far[np.random.randint(len(far))]
    return np.exp2(a.ravel()).repeat(32)


BF16 = ml_dtypes.bfloat16


def bf(x):
    return np.asarray(x, np.float32).astype(BF16)


def f64(x):
    return np.asarray(x).astype(np.float64)


T, D, F, E, R = 1024, 1024, 1024, 128, 512


def softmax_last(l):
    m = np.max(l, axis=-1, keepdims=True)
    p = np.exp(l - m)
    return p / np.sum(p, axis=-1, keepdims=True)


def draw0():
    s, t = mx_kscale(D), mx_kscale(R)
    sd, sr = np.sqrt(D), np.sqrt(R)
    return {
        "x": bf(np.random.standard_normal((T, D)) * s),
        "w0": bf(np.random.standard_normal((D, F)) / sd / s[:, None]),
        "wr": bf(np.random.standard_normal((D, E)) / sd / s[:, None]),
        "br": bf(np.random.standard_normal(E) * 0.5),
        "a": bf(np.random.standard_normal((D, R)) / sd / s[:, None] * t),
        "b": bf(np.random.standard_normal((R, F)) * 0.6 / sr / t[:, None]),
    }


def core(x, w0, wr, br, a, b):
    n_tok = x.shape[0]
    n_exp = wr.shape[1]
    rank = a.shape[1]
    per_exp = rank // n_exp
    xq = mxq(f64(x), 1, "e4m3")
    l = (xq @ mxq(f64(wr), 0, "e4m3")) + f64(br)
    g = float(n_exp) * softmax_last(l)
    u = xq @ mxq(f64(a), 0, "e4m3")
    z = u.reshape(n_tok, n_exp, per_exp) * g[:, :, None]
    z = z.reshape(n_tok, rank)
    y = (xq @ mxq(f64(w0), 0, "e4m3")) + (mxq(z, 1, "e4m3") @ mxq(f64(b), 0, "e4m3"))
    return y


def e4m3fn_bytes(y):
    return np.clip(np.asarray(y, np.float64), -448.0, 448.0).astype(np.float32).astype(ml_dtypes.float8_e4m3fn).view(np.uint8)


def e4m3fn_values(b):
    return np.asarray(b, np.uint8).view(ml_dtypes.float8_e4m3fn).astype(np.float64)


def setup_inputs():
    d = draw0()
    x0 = np.asarray(d['x']).astype(np.float64)
    s = (np.max(np.abs(x0), axis=(0,), keepdims=True) / 448.0).astype(np.float32)
    out = {}
    for k, v in d.items():
        if k == 'x':
            out['x_bytes'] = e4m3fn_bytes(x0 / s.astype(np.float64))
            out['x_scale'] = s
        else:
            out[k] = v
    return out


def reference(x_bytes, x_scale, w0, wr, br, a, b):
    return core(e4m3fn_values(x_bytes) * x_scale.astype(np.float64), w0, wr, br, a, b)

@@ -1,0 +1,319 @@
+from contextlib import ExitStack
+
+import concourse.mybir as mybir
+from concourse.masks import make_identity
+
+T, D, F, E, R = 1024, 1024, 1024, 128, 512
+P = 128
+FLOPS = 2 * T * (D * (F + E + R) + R * F)
+
+F32 = mybir.dt.float32
+BF16 = mybir.dt.bfloat16
+U32 = mybir.dt.uint32
+U8 = mybir.dt.uint8
+FP8 = mybir.dt.float8_e4m3fn
+FP8X4 = mybir.dt.float8_e4m3fn_x4
+ALU = mybir.AluOpType
+ACT = mybir.ActivationFunctionType
+
+ORDER = """
+Ia0.1 Ia0.0 Bc Iwr.0 Sc1 Sc0 Ib0.1 Qa0 W2 Ib0.0 Qwr X2 W0 Iw10.1
+W1 X0 Iw00.0 Iw10.0 C0 W3 Ib1.0 X1 Qw10 q0 C2 W6 l0 C1
+X3 Ia1.1 q2 X6 q1 l2 Ia1.0 l1 C3 sA0 Iw00.1 Qa1 sM0 u1
+q3 sE0 Qw00 u0 Iw01.1 sN0 l3 o0.0 Qb0 o2.0 Ib1.1 W5 sT0 o1.0
+sA1 C6 W4 sC0 X5 Iw11.0 sM1 X4 z0 sE1 z1 u3 C5 sN1
+C4 u2 k1 W7 Iw01.0 p1.0 sT1 q5 X7 k0 sC1 q4 p0.0 e1.0
+z2 l4 l5 e0.0 D1.0 o3.0 z3 Iw11.1 u4 D0.0 Qw01 u5 k2 q6
+C7 k3 p2.0 Qw11 p3.0 e2.0 o4.0 Qb1 e3.0 l6 D2.0 o2.1 q7 D3.0
+sA2 p2.1 l7 o0.1 e2.1 sM2 sA3 p0.1 sE2 D2.1 o1.1 sM3 e0.1 sN2
+p1.1 sE3 D0.1 o3.1 e1.1 p3.1 sN3 D1.1 sT2 e3.1 sT3 sC2 o5.1 sC3
+z4 D3.1 o5.0 z5 u6 k4 k5 p4.0 z6 p5.1 e4.0 u7 k6 e5.1
+D4.0 p5.0 z7 o7.1 e5.0 D5.1 o4.1 k7 D5.0 p7.1 p4.1 e7.1 o7.0 e4.1
+p7.0 D7.1 o6.0 e7.0 D4.1 p6.0 o6.1 D7.0 e6.0 p6.1 D6.0 e6.1 D6.1
+""".split()
+ON_V = set("Ia0.1 Iwr.0 Sc0 Iw10.0 Ia1.0 e1.1 e3.1 e7.1 e7.0".split())
+
+
+def tile_rankwisemoloradenserouter_kernel(tc, x_bytes, x_scale, w0, wr, br, a, b, out):
+    nc = tc.nc
+    with ExitStack() as ctx:
+        keep = ctx.enter_context(tc.tile_pool(name="keep", bufs=1))
+        psum = ctx.enter_context(tc.psum_pool(name="psum", bufs=1))
+
+        def sb(name, shape, dtype):
+            return keep.tile(shape, dtype, name=name, tag=name, align_bytes=64)
+
+        def bank(tag, bufs, shape):
+            return psum.tile(shape, F32, name=tag, tag=tag, bufs=bufs)
+
+        ident = sb("ident", [P, P], F32)
+        warm = sb("warm", [P, 1], F32)
+        scol = sb("scol", [P, 2, 4], F32)
+        srow = sb("srow", [P, 2, P, 4], F32)
+        xr = sb("xr", [P, 8, D], U8)
+        xb = sb("xb", [P, 8, D], BF16)
+        xg = sb("xg", [P, 8, 4 * 2 * P], BF16)
+        xc = sb("xc", [P, 8, 2 * P], U32)
+        xs = sb("xs", [P, 8, 2 * P], U8)
+        brb = sb("brb", [P, E], BF16)
+        gT = sb("gT", [P, 8 * P], F32)
+        zg = sb("zg", [P, 8, P * 4], BF16)
+        zc = sb("zc", [P, 8, P], U32)
+        zs = sb("zs", [P, 8, P], U8)
+        osb = sb("osb", [P, 8, F], F32)
+        raw, grp, cod, scl = {}, {}, {}, {}
+        for k in ("a0", "a1", "b0", "b1", "w00", "w10", "w01", "w11"):
+            raw[k] = sb("raw_" + k, [P, 4, 512], BF16)
+            grp[k] = sb("grp_" + k, [P, 512 * 4], BF16)
+            cod[k] = sb("cod_" + k, [P, 512], U32)
+            scl[k] = sb("scl_" + k, [P, 512], U8)
+        raw["wr"] = sb("raw_wr", [P, 2, 4, E], BF16)
+        grp["wr"] = sb("grp_wr", [P, 2 * E * 4], BF16)
+        cod["wr"] = sb("cod_wr", [P, 2 * E], U32)
+        scl["wr"] = sb("scl_wr", [P, 2 * E], U8)
+        nl = [sb("nl%d" % h, [P, 2, E], F32) for h in range(4)]
+        nm = [sb("nm%d" % h, [P, 2], F32) for h in range(4)]
+        ss = [sb("ss%d" % h, [P, 2], F32) for h in range(4)]
+        rs = [sb("rs%d" % h, [P, 2], F32) for h in range(4)]
+        ex = [sb("ex%d" % h, [P, 2, E], F32) for h in range(4)]
+        gn = [sb("gn%d" % h, [P, 2, E], F32) for h in range(4)]
+
+        x_v = x_bytes.rearrange("(p i) k -> p i k", i=8)
+        out_v = out.rearrange("(p i) f -> p i f", i=8)
+        wr_v = wr.rearrange("(g p j) e -> p g j e", p=P, j=4)
+        a_v = a.rearrange("(g p j) r -> g p j r", p=P, j=4)
+        w0_v = w0.rearrange("(g p j) f -> g p j f", p=P, j=4)
+        b_v = b.rearrange("(p j) f -> p j f", j=4)
+        banks = {}
+
+        def load(key):
+            if key == "v":
+                nc.sync.dma_start(out=scol[:], in_=x_scale.rearrange("o (g p t) -> p (o g) t", p=P, t=4))
+            elif key == "br":
+                nc.scalar.dma_start(out=brb[:], in_=br.partition_broadcast(P))
+            elif key[0] == "x":
+                i0, i1 = int(key[1]), int(key[2]) + 1
+                nc.sync.dma_start(out=xr[:, i0:i1, :], in_=x_v[:, i0:i1, :])
+            elif key == "wr":
+                nc.sync.dma_start(out=raw["wr"][:], in_=wr_v)
+            elif key[0] == "a":
+                nc.sync.dma_start(out=raw[key][:], in_=a_v[int(key[1])])
+            elif key[0] == "b":
+                n = int(key[1])
+                nc.sync.dma_start(out=raw[key][:], in_=b_v[:, :, 512 * n : 512 * n + 512])
+            else:
+                g, n = int(key[1]), int(key[2])
+                nc.sync.dma_start(out=raw[key][:], in_=w0_v[g][:, :, 512 * n : 512 * n + 512])
+
+        def copy(step, out_ap, in_ap):
+            if step in ON_V:
+                nc.vector.tensor_copy(out=out_ap, in_=in_ap)
+            else:
+                nc.scalar.copy(out=out_ap, in_=in_ap)
+
+        def spread(step):
+            for g in range(2):
+                banks["B%d" % g] = bank("tr", 2, [P, 4, P])
+                for t in range(4):
+                    nc.tensor.transpose(banks["B%d" % g][:, t, :], scol[:, g, t : t + 1].to_broadcast([P, P]), ident[:])
+
+        def spread_out(step):
+            g = int(step[2])
+            copy(step, srow[:, g], banks["B%d" % g][:].rearrange("p t n -> p n t"))
+
+        def widen(step):
+            i = int(step[1])
+            halves = 2 if i == 0 else 1
+            w = D // halves
+            flat = srow[:].rearrange("p g n t -> p (g n t)")
+            for h in range(halves):
+                c = slice(h * w, h * w + w)
+                nc.vector.tensor_tensor(out=xb[:, i, c], in0=xr[:, i, c].bitcast(FP8), in1=flat[:, c], op=ALU.mult)
+
+        def turn(step):
+            i = int(step[1])
+            banks[step] = bank("tr", 2, [P, 4, P])
+            words = xb[:, i, :].bitcast(F32)
+            for g in range(2):
+                for u in range(2):
+                    nc.tensor.transpose(banks[step][:, 2 * g + u, :], words[:, 256 * g + u : 256 * (g + 1) : 2], ident[:])
+
+        def turn_out(step):
+            i = int(step[1])
+            copy(
+                step,
+                xg[:, i, :].bitcast(F32).rearrange("p (g r u) -> p g r u", g=2, u=2),
+                banks["X%d" % i][:].rearrange("p (g u) r -> p g r u", u=2),
+            )
+
+        def xquant(step):
+            i = int(step[1])
+            nc.vector.quantize_mx(out=xc[:, i, :].bitcast(FP8X4), scales=xs[:, i, :], in_=xg[:, i, :])
+
+        def inter(step):
+            key, h = step[1:].split(".")
+            h = int(h)
+            if key == "wr":
+                for g in range(2):
+                    copy(
+                        step,
+                        grp["wr"][:, 512 * g : 512 * g + 512].rearrange("p (c i j) -> p c j i", i=4, j=4),
+                        raw["wr"][:, g].rearrange("p j (c i) -> p c j i", i=4),
+                    )
+            elif key[0] == "a":
+                m = slice(64 * h, 64 * h + 64)
+                copy(
+                    step,
+                    grp[key][:].rearrange("p (t m j) -> p t m j", t=4, j=4)[:, :, m, :],
+                    raw[key][:].rearrange("p j (m t) -> p t m j", t=4)[:, :, m, :],
+                )
+            else:
+                c = slice(64 * h, 64 * h + 64)
+                copy(
+                    step,
+                    grp[key][:].rearrange("p (c i j) -> p c j i", i=4, j=4)[:, c],
+                    raw[key][:].rearrange("p j (c i) -> p c j i", i=4)[:, c],
+                )
+
+        def wquant(step):
+            k = step[1:]
+            nc.vector.quantize_mx(out=cod[k][:].bitcast(FP8X4), scales=scl[k][:], in_=grp[k][:])
+
+        def mx(out_ap, lc, ls, rc, rsc, start, stop):
+            nc.tensor.matmul_mx(
+                out=out_ap, lhsT=lc.bitcast(FP8X4), lhsT_scale=ls, rhs=rc.bitcast(FP8X4), rhs_scale=rsc, start=start, stop=stop
+            )
+
+        def logits(step):
+            i = int(step[1])
+            if "L%d" % (i // 4) not in banks:
+                banks["L%d" % (i // 4)] = bank("lg", 1, [P, 4, E])
+            for g in range(2):
+                c = slice(P * g, P * g + P)
+                mx(banks["L%d" % (i // 4)][:, i % 4, :], xc[:, i, c], xs[:, i, c], cod["wr"][:, c], scl["wr"][:, c], g == 0, g == 1)
+
+        def down(step):
+            i = int(step[1])
+            banks[step] = bank("u", 2, [P, 4, P])
+            for t in range(4):
+                m = slice(P * t, P * t + P)
+                for g in range(2):
+                    c = slice(P * g, P * g + P)
+                    k = "a%d" % g
+                    mx(banks[step][:, t, :], cod[k][:, m], scl[k][:, m], xc[:, i, c], xs[:, i, c], g == 0, g == 1)
+
+        def soft_add(step):
+            h = int(step[2])
+            nc.vector.scalar_tensor_tensor(
+                out=nl[h][:],
+                in0=banks["L%d" % (h // 2)][:, 2 * (h % 2) : 2 * (h % 2) + 2, :],
+                scalar=-1.0,
+                in1=brb[:].unsqueeze(1).to_broadcast([P, 2, E]),
+                op0=ALU.mult,
+                op1=ALU.subtract,
+            )
+
+        def soft_min(step):
+            h = int(step[2])
+            nc.vector.tensor_reduce(out=nm[h][:], in_=nl[h][:], axis=mybir.AxisListType.X, op=ALU.min)
+
+        def soft_exp(step):
+            h = int(step[2])
+            for j in range(2):
+                nc.scalar.activation(
+                    out=ex[h][:, j, :],
+                    in_=nl[h][:, j, :],
+                    func=ACT.Exp,
+                    bias=nm[h][:, j : j + 1],
+                    scale=-1.0,
+                    accum_out=ss[h][:, j : j + 1],
+                )
+
+        def soft_norm(step):
+            h = int(step[2])
+            nc.vector.reciprocal(out=rs[h][:], in_=ss[h][:])
+            for j in range(2):
+                nc.vector.tensor_scalar(
+                    out=gn[h][:, j, :], in0=ex[h][:, j, :], scalar1=rs[h][:, j : j + 1], scalar2=float(E), op0=ALU.mult, op1=ALU.mult
+                )
+
+        def soft_turn(step):
+            h = int(step[2])
+            banks[step] = bank("tr", 2, [P, 2, P])
+            for j in range(2):
+                nc.tensor.transpose(banks[step][:, j, :], gn[h][:, j, :], ident[:])
+
+        def soft_out(step):
+            h = int(step[2])
+            copy(step, gT[:, 256 * h : 256 * h + 256], banks["sT%d" % h][:].rearrange("p j n -> p (j n)"))
+
+        def zmul(step):
+            i = int(step[1])
+            nc.vector.tensor_tensor(
+                out=zg[:, i, :].rearrange("p (n t) -> p n t", t=4),
+                in0=banks["u%d" % i][:].rearrange("p t n -> p n t"),
+                in1=gT[:, P * i : P * i + P].unsqueeze(2).to_broadcast([P, P, 4]),
+                op=ALU.mult,
+            )
+
+        def zquant(step):
+            i = int(step[1])
+            nc.vector.quantize_mx(out=zc[:, i, :].bitcast(FP8X4), scales=zs[:, i, :], in_=zg[:, i, :])
+
+        def base(step):
+            i, n = int(step[1]), step[3]
+            banks[step[1:]] = bank("o", 3, [P, 512])
+            for g in range(2):
+                c = slice(P * g, P * g + P)
+                k = "w%d%s" % (g, n)
+                mx(banks[step[1:]][:], xc[:, i, c], xs[:, i, c], cod[k][:], scl[k][:], g == 0, False)
+
+        def up(step):
+            i, n = int(step[1]), step[3]
+            k = "b" + n
+            mx(banks[step[1:]][:], zc[:, i, :], zs[:, i, :], cod[k][:], scl[k][:], False, True)
+
+        def evac(step):
+            i, n = int(step[1]), int(step[3])
+            copy(step, osb[:, i, 512 * n : 512 * n + 512], banks[step[1:]][:])
+
+        def store(step):
+            i, n = int(step[1]), int(step[3])
+            nc.sync.dma_start(out=out_v[:, i, 512 * n : 512 * n + 512], in_=osb[:, i, 512 * n : 512 * n + 512])
+
+        steps = {
+            "Bc": spread,
+            "Sc": spread_out,
+            "W": widen,
+            "X": turn,
+            "C": turn_out,
+            "q": xquant,
+            "I": inter,
+            "Q": wquant,
+            "l": logits,
+            "u": down,
+            "sA": soft_add,
+            "sM": soft_min,
+            "sE": soft_exp,
+            "sN": soft_norm,
+            "sT": soft_turn,
+            "sC": soft_out,
+            "z": zmul,
+            "k": zquant,
+            "o": base,
+            "p": up,
+            "e": evac,
+            "D": store,
+        }
+
+        make_identity(nc, ident[:])
+        nc.vector.memset(warm[:], 0.0)
+        with tc.manual_schedule():
+            nc.scalar.activation(out=warm[:], in_=warm[:], func=ACT.Exp)
+            for key in "a0 v br wr b0 x23 w10 x01 w00 b1 x47 a1 w11 w01".split():
+                load(key)
+            for step in ORDER:
+                fn = steps.get(step[:2])
+                if fn is None:
+                    fn = steps[step[0]]
+                fn(step)

@@ -17,21 +17,22 @@ ALU = mybir.AluOpType
 ACT = mybir.ActivationFunctionType
 
 ORDER = """
-Ia0.1 Ia0.0 Bc Iwr.0 Sc1 Sc0 Ib0.1 Qa0 W2 Ib0.0 Qwr X2 W0 Iw10.1
-W1 X0 Iw00.0 Iw10.0 C0 W3 Ib1.0 X1 Qw10 q0 C2 W6 l0 C1
-X3 Ia1.1 q2 X6 q1 l2 Ia1.0 l1 C3 sA0 Iw00.1 Qa1 sM0 u1
-q3 sE0 Qw00 u0 Iw01.1 sN0 l3 o0.0 Qb0 o2.0 Ib1.1 W5 sT0 o1.0
-sA1 C6 W4 sC0 X5 Iw11.0 sM1 X4 z0 sE1 z1 u3 C5 sN1
-C4 u2 k1 W7 Iw01.0 p1.0 sT1 q5 X7 k0 sC1 q4 p0.0 e1.0
-z2 l4 l5 e0.0 D1.0 o3.0 z3 Iw11.1 u4 D0.0 Qw01 u5 k2 q6
-C7 k3 p2.0 Qw11 p3.0 e2.0 o4.0 Qb1 e3.0 l6 D2.0 o2.1 q7 D3.0
-sA2 p2.1 l7 o0.1 e2.1 sM2 sA3 p0.1 sE2 D2.1 o1.1 sM3 e0.1 sN2
-p1.1 sE3 D0.1 o3.1 e1.1 p3.1 sN3 D1.1 sT2 e3.1 sT3 sC2 o5.1 sC3
-z4 D3.1 o5.0 z5 u6 k4 k5 p4.0 z6 p5.1 e4.0 u7 k6 e5.1
-D4.0 p5.0 z7 o7.1 e5.0 D5.1 o4.1 k7 D5.0 p7.1 p4.1 e7.1 o7.0 e4.1
-p7.0 D7.1 o6.0 e7.0 D4.1 p6.0 o6.1 D7.0 e6.0 p6.1 D6.0 e6.1 D6.1
+Bc Sc0 Sc1 Ia1.0 W1 Ia1.1 W0 X1 Iw10.0 Qa1 X0 W3 Iw11.0 W6
+Iw10.1 W5 C0 W2 Iw11.1 X3 q0 C1 Iw00.1 Ia0.0 X5 q1 Iwr.0 C5
+Iw00.0 Iw01.1 X2 Qwr W4 l0 l1 C3 Qw00 C2 X6 q3 Ia0.1 X4
+q2 sA0 l3 Qw10 l2 C6 sM0 o1.0 C4 sA1 Ib0.1 o3.0 sE0 o0.0
+Ib1.1 sM1 sR0 Qa0 sN0 q4 Iw01.0 u0 q5 W7 sT0 u1 sE1 sC0
+Qw11 l4 X7 Ib0.0 sR1 z1 l5 sN1 z0 u2 Ib1.0 sA2 sT1 Qb0
+u3 sC1 k0 C7 sM2 p0.0 z2 p1.0 sE2 z3 e0.0 u4 e1.0 q6
+u5 D0.0 sR2 k1 o2.0 sN2 D1.0 Qw01 p3.0 q7 p2.0 l6 e3.0 Qb1
+sT2 l7 e2.0 D3.0 o5.0 sC2 sA3 o3.1 D2.0 z5 o0.1 sM3 p3.1 z4
+u6 sE3 e3.1 sR3 p0.1 k2 u7 sN3 e0.1 D3.1 o5.1 D0.1 p5.0 p5.1
+sT3 e5.0 e5.1 o4.1 sC3 D5.0 o4.0 z6 D5.1 p4.1 p4.0 z7 o2.1 e4.1
+e4.0 p2.1 D4.1 o6.1 k3 e2.1 o1.1 D4.0 p6.1 D2.1 p1.1 o6.0 e6.1 e1.1
+p6.0 D6.1 o7.0 e6.0 p7.0 D1.1 o7.1 e7.0 D6.0 p7.1 D7.0 e7.1 D7.1
 """.split()
-ON_V = set("Ia0.1 Iwr.0 Sc0 Iw10.0 Ia1.0 e1.1 e3.1 e7.1 e7.0".split())
+FIRST_W = [s for s in ORDER if s[0] == "W"][0]
+ON_V = set("Sc0 Iw00.1 Iwr.0 Iw00.0 Ib0.1 e2.0 e5.0 sC3 e4.0 e1.1 e6.0".split())
 
 
 def tile_rankwisemoloradenserouter_kernel(tc, x_bytes, x_scale, w0, wr, br, a, b, out):
@@ -62,8 +63,14 @@ def tile_rankwisemoloradenserouter_kernel(tc, x_bytes, x_scale, w0, wr, br, a, b
         zs = sb("zs", [P, 8, P], U8)
         osb = sb("osb", [P, 8, F], F32)
         raw, grp, cod, scl = {}, {}, {}, {}
+        rawb = sb("raw_b", [P, 4, F], BF16)
+        raww = [sb("raw_w%d" % g, [P, 4, F], BF16) for g in range(2)]
         for k in ("a0", "a1", "b0", "b1", "w00", "w10", "w01", "w11"):
-            raw[k] = sb("raw_" + k, [P, 4, 512], BF16)
+            if k[0] == "a":
+                raw[k] = sb("raw_" + k, [P, 4, 512], BF16)
+            else:
+                n = int(k[-1])
+                raw[k] = (rawb if k[0] == "b" else raww[int(k[1])])[:, :, 512 * n : 512 * n + 512]
             grp[k] = sb("grp_" + k, [P, 512 * 4], BF16)
             cod[k] = sb("cod_" + k, [P, 512], U32)
             scl[k] = sb("scl_" + k, [P, 512], U8)
@@ -98,12 +105,10 @@ def tile_rankwisemoloradenserouter_kernel(tc, x_bytes, x_scale, w0, wr, br, a, b
                 nc.sync.dma_start(out=raw["wr"][:], in_=wr_v)
             elif key[0] == "a":
                 nc.sync.dma_start(out=raw[key][:], in_=a_v[int(key[1])])
-            elif key[0] == "b":
-                n = int(key[1])
-                nc.sync.dma_start(out=raw[key][:], in_=b_v[:, :, 512 * n : 512 * n + 512])
+            elif key == "b":
+                nc.sync.dma_start(out=rawb[:], in_=b_v)
             else:
-                g, n = int(key[1]), int(key[2])
-                nc.sync.dma_start(out=raw[key][:], in_=w0_v[g][:, :, 512 * n : 512 * n + 512])
+                nc.sync.dma_start(out=raww[int(key[1])][:], in_=w0_v[int(key[1])])
 
         def copy(step, out_ap, in_ap):
             if step in ON_V:
@@ -123,7 +128,7 @@ def tile_rankwisemoloradenserouter_kernel(tc, x_bytes, x_scale, w0, wr, br, a, b
 
         def widen(step):
             i = int(step[1])
-            halves = 2 if i == 0 else 1
+            halves = 2 if step == FIRST_W else 1
             w = D // halves
             flat = srow[:].rearrange("p g n t -> p (g n t)")
             for h in range(halves):
@@ -172,7 +177,7 @@ def tile_rankwisemoloradenserouter_kernel(tc, x_bytes, x_scale, w0, wr, br, a, b
                 copy(
                     step,
                     grp[key][:].rearrange("p (c i j) -> p c j i", i=4, j=4)[:, c],
-                    raw[key][:].rearrange("p j (c i) -> p c j i", i=4)[:, c],
+                    raw[key].rearrange("p j (c i) -> p c j i", i=4)[:, c],
                 )
 
         def wquant(step):
@@ -229,11 +234,14 @@ def tile_rankwisemoloradenserouter_kernel(tc, x_bytes, x_scale, w0, wr, br, a, b
                     accum_out=ss[h][:, j : j + 1],
                 )
 
-        def soft_norm(step):
+        def soft_recip(step):
             h = int(step[2])
             nc.vector.reciprocal(out=rs[h][:], in_=ss[h][:])
+
+        def soft_norm(step):
+            h = int(step[2])
             for j in range(2):
-                nc.vector.tensor_scalar(
+                nc.gpsimd.tensor_scalar(
                     out=gn[h][:, j, :], in0=ex[h][:, j, :], scalar1=rs[h][:, j : j + 1], scalar2=float(E), op0=ALU.mult, op1=ALU.mult
                 )
 
@@ -257,8 +265,12 @@ def tile_rankwisemoloradenserouter_kernel(tc, x_bytes, x_scale, w0, wr, br, a, b
             )
 
         def zquant(step):
-            i = int(step[1])
-            nc.vector.quantize_mx(out=zc[:, i, :].bitcast(FP8X4), scales=zs[:, i, :], in_=zg[:, i, :])
+            c = slice(2 * int(step[1]), 2 * int(step[1]) + 2)
+            nc.vector.quantize_mx(
+                out=zc[:, c, :].rearrange("p i n -> p (i n)").bitcast(FP8X4),
+                scales=zs[:, c, :].rearrange("p i n -> p (i n)"),
+                in_=zg[:, c, :].rearrange("p i n -> p (i n)"),
+            )
 
         def base(step):
             i, n = int(step[1]), step[3]
@@ -295,6 +307,7 @@ def tile_rankwisemoloradenserouter_kernel(tc, x_bytes, x_scale, w0, wr, br, a, b
             "sA": soft_add,
             "sM": soft_min,
             "sE": soft_exp,
+            "sR": soft_recip,
             "sN": soft_norm,
             "sT": soft_turn,
             "sC": soft_out,
@@ -310,7 +323,7 @@ def tile_rankwisemoloradenserouter_kernel(tc, x_bytes, x_scale, w0, wr, br, a, b
         nc.vector.memset(warm[:], 0.0)
         with tc.manual_schedule():
             nc.scalar.activation(out=warm[:], in_=warm[:], func=ACT.Exp)
-            for key in "a0 v br wr b0 x23 w10 x01 w00 b1 x47 a1 w11 w01".split():
+            for key in "v x01 br a1 w1 x23 x47 a0 w0 wr b".split():
                 load(key)
             for step in ORDER:
                 fn = steps.get(step[:2])

@@ -17,22 +17,24 @@ ALU = mybir.AluOpType
 ACT = mybir.ActivationFunctionType
 
 ORDER = """
-Bc Sc0 Sc1 Ia1.0 W1 Ia1.1 W0 X1 Iw10.0 Qa1 X0 W3 Iw11.0 W6
-Iw10.1 W5 C0 W2 Iw11.1 X3 q0 C1 Iw00.1 Ia0.0 X5 q1 Iwr.0 C5
-Iw00.0 Iw01.1 X2 Qwr W4 l0 l1 C3 Qw00 C2 X6 q3 Ia0.1 X4
-q2 sA0 l3 Qw10 l2 C6 sM0 o1.0 C4 sA1 Ib0.1 o3.0 sE0 o0.0
-Ib1.1 sM1 sR0 Qa0 sN0 q4 Iw01.0 u0 q5 W7 sT0 u1 sE1 sC0
-Qw11 l4 X7 Ib0.0 sR1 z1 l5 sN1 z0 u2 Ib1.0 sA2 sT1 Qb0
-u3 sC1 k0 C7 sM2 p0.0 z2 p1.0 sE2 z3 e0.0 u4 e1.0 q6
-u5 D0.0 sR2 k1 o2.0 sN2 D1.0 Qw01 p3.0 q7 p2.0 l6 e3.0 Qb1
-sT2 l7 e2.0 D3.0 o5.0 sC2 sA3 o3.1 D2.0 z5 o0.1 sM3 p3.1 z4
-u6 sE3 e3.1 sR3 p0.1 k2 u7 sN3 e0.1 D3.1 o5.1 D0.1 p5.0 p5.1
-sT3 e5.0 e5.1 o4.1 sC3 D5.0 o4.0 z6 D5.1 p4.1 p4.0 z7 o2.1 e4.1
-e4.0 p2.1 D4.1 o6.1 k3 e2.1 o1.1 D4.0 p6.1 D2.1 p1.1 o6.0 e6.1 e1.1
-p6.0 D6.1 o7.0 e6.0 p7.0 D1.1 o7.1 e7.0 D6.0 p7.1 D7.0 e7.1 D7.1
+Bc Iwr.0 Iwr.1 Sc0 Sc1 Qwr W0 bv Ia1.0 W1 X0 Ia1.2 Ia1.1 W3
+X1 bt C0 Ia1.3 W2 X3 C1 bs q0 Ia0.1 X2 q1 W5 l0
+Ia0.0 l1 C3 W4 C2 X5 Ia0.2 sA0 X4 Ib0.1 Qa1 Ia0.3 sM0 q3
+C5 Qa0 l3 C4 q2 u0 q5 sE0 q4 l2 Iw11.0 l5 sR0 l4
+W6 u3 Ib0.0 Iw10.3 sA1 X6 Iw10.1 Ib0.2 z0 Ib0.3 Iw00.0 u1 Iw10.2 W7
+Iw10.0 sM1 Iw00.2 X7 z1 Iw00.3 Iw00.1 Qw10 C6 sA2 sE1 Y0 Qw00 Ib1.3
+u2 sR1 H0 sM2 o0.0 q6 Iw11.3 o3.0 z2 sE2 o1.0 z3 C7 u4
+sR2 k0 Ib1.2 Y1 Qb0 Iw11.2 u5 z4 Iw01.2 p0.0 q7 u6 Iw11.1 H1
+l6 z5 p1.0 e0.0 l7 Ib1.0 Iw01.0 k1 o2.0 D0.0  Iw01.3 Y2 Iw01.1 Qw11
+p2.0 e1.0 Qw01 u7 Ib1.1 D1.0 p3.0 o2.1 e2.0 Qb1 H2 o1.1 D2.0 e3.0
+p2.1 sA3 o4.0 D3.0 k2 e2.1 p1.1 sM3 p4.0 o5.1 e1.1 sE3 e4.0 p5.1
+sR3 o5.0 e5.1 z7 D4.0 o4.1 z6 D1.1 p5.0 p4.1 o0.1 e5.0 D5.1 Y3
+e4.1 D5.0 p0.1 D2.1 H3 o3.1 D4.1 e0.1 o6.0 k3 p3.1 D0.1 o7.0 e3.1
+p6.0 p7.0 D3.1 o7.1 e6.0 e7.0 p7.1 D6.0 o6.1 e7.1 p6.1 D7.0 e6.1 D7.1
+D6.1
 """.split()
 FIRST_W = [s for s in ORDER if s[0] == "W"][0]
-ON_V = set("Sc0 Iw00.1 Iwr.0 Iw00.0 Ib0.1 e2.0 e5.0 sC3 e4.0 e1.1 e6.0".split())
+ON_V = set("Iwr.1 Sc0 Iw10.1 Iw00.0 Iw00.1 Iw11.1 Ib1.0 Iw01.3 e3.0 e1.1 e7.0 e7.1".split())
 
 
 def tile_rankwisemoloradenserouter_kernel(tc, x_bytes, x_scale, w0, wr, br, a, b, out):
@@ -56,8 +58,10 @@ def tile_rankwisemoloradenserouter_kernel(tc, x_bytes, x_scale, w0, wr, br, a, b
         xg = sb("xg", [P, 8, 4 * 2 * P], BF16)
         xc = sb("xc", [P, 8, 2 * P], U32)
         xs = sb("xs", [P, 8, 2 * P], U8)
-        brb = sb("brb", [P, E], BF16)
-        gT = sb("gT", [P, 8 * P], F32)
+        brc = sb("brc", [P, 1], BF16)
+        brf = sb("brf", [P, 1], F32)
+        brb = sb("brb", [P, E], F32)
+        zb = sb("zb", [P, 8, R], BF16)
         zg = sb("zg", [P, 8, P * 4], BF16)
         zc = sb("zc", [P, 8, P], U32)
         zs = sb("zs", [P, 8, P], U8)
@@ -83,7 +87,7 @@ def tile_rankwisemoloradenserouter_kernel(tc, x_bytes, x_scale, w0, wr, br, a, b
         ss = [sb("ss%d" % h, [P, 2], F32) for h in range(4)]
         rs = [sb("rs%d" % h, [P, 2], F32) for h in range(4)]
         ex = [sb("ex%d" % h, [P, 2, E], F32) for h in range(4)]
-        gn = [sb("gn%d" % h, [P, 2, E], F32) for h in range(4)]
+        sd = [sb("sd%d" % h, [P, 2], F32) for h in range(4)]
 
         x_v = x_bytes.rearrange("(p i) k -> p i k", i=8)
         out_v = out.rearrange("(p i) f -> p i f", i=8)
@@ -97,7 +101,7 @@ def tile_rankwisemoloradenserouter_kernel(tc, x_bytes, x_scale, w0, wr, br, a, b
             if key == "v":
                 nc.sync.dma_start(out=scol[:], in_=x_scale.rearrange("o (g p t) -> p (o g) t", p=P, t=4))
             elif key == "br":
-                nc.scalar.dma_start(out=brb[:], in_=br.partition_broadcast(P))
+                nc.sync.dma_start(out=brc[:], in_=br.rearrange("(p o) -> p o", o=1))
             elif key[0] == "x":
                 i0, i1 = int(key[1]), int(key[2]) + 1
                 nc.sync.dma_start(out=xr[:, i0:i1, :], in_=x_v[:, i0:i1, :])
@@ -121,6 +125,16 @@ def tile_rankwisemoloradenserouter_kernel(tc, x_bytes, x_scale, w0, wr, br, a, b
                 banks["B%d" % g] = bank("tr", 2, [P, 4, P])
                 for t in range(4):
                     nc.tensor.transpose(banks["B%d" % g][:, t, :], scol[:, g, t : t + 1].to_broadcast([P, P]), ident[:])
+
+        def bias_cast(step):
+            nc.vector.tensor_copy(out=brf[:], in_=brc[:])
+
+        def bias_spread(step):
+            banks["br"] = bank("lg", 1, [P, P])
+            nc.tensor.transpose(banks["br"][:], brf[:].to_broadcast([P, P]), ident[:])
+
+        def bias_out(step):
+            nc.scalar.copy(out=brb[:], in_=banks["br"][:])
 
         def spread_out(step):
             g = int(step[2])
@@ -159,26 +173,11 @@ def tile_rankwisemoloradenserouter_kernel(tc, x_bytes, x_scale, w0, wr, br, a, b
             key, h = step[1:].split(".")
             h = int(h)
             if key == "wr":
-                for g in range(2):
-                    copy(
-                        step,
-                        grp["wr"][:, 512 * g : 512 * g + 512].rearrange("p (c i j) -> p c j i", i=4, j=4),
-                        raw["wr"][:, g].rearrange("p j (c i) -> p c j i", i=4),
-                    )
-            elif key[0] == "a":
-                m = slice(64 * h, 64 * h + 64)
-                copy(
-                    step,
-                    grp[key][:].rearrange("p (t m j) -> p t m j", t=4, j=4)[:, :, m, :],
-                    raw[key][:].rearrange("p j (m t) -> p t m j", t=4)[:, :, m, :],
-                )
+                src = raw["wr"][:, h]
             else:
-                c = slice(64 * h, 64 * h + 64)
-                copy(
-                    step,
-                    grp[key][:].rearrange("p (c i j) -> p c j i", i=4, j=4)[:, c],
-                    raw[key].rearrange("p j (c i) -> p c j i", i=4)[:, c],
-                )
+                src = raw[key][:, :, P * h : P * h + P]
+            dst = grp[key][:, 512 * h : 512 * h + 512]
+            copy(step, dst.rearrange("p (c j) -> p c j", j=4), src.rearrange("p j c -> p c j"))
 
         def wquant(step):
             k = step[1:]
@@ -199,13 +198,11 @@ def tile_rankwisemoloradenserouter_kernel(tc, x_bytes, x_scale, w0, wr, br, a, b
 
         def down(step):
             i = int(step[1])
-            banks[step] = bank("u", 2, [P, 4, P])
-            for t in range(4):
-                m = slice(P * t, P * t + P)
-                for g in range(2):
-                    c = slice(P * g, P * g + P)
-                    k = "a%d" % g
-                    mx(banks[step][:, t, :], cod[k][:, m], scl[k][:, m], xc[:, i, c], xs[:, i, c], g == 0, g == 1)
+            banks[step] = bank("u", 2, [P, R])
+            for g in range(2):
+                c = slice(P * g, P * g + P)
+                k = "a%d" % g
+                mx(banks[step][:], xc[:, i, c], xs[:, i, c], cod[k][:], scl[k][:], g == 0, g == 1)
 
         def soft_add(step):
             h = int(step[2])
@@ -236,32 +233,35 @@ def tile_rankwisemoloradenserouter_kernel(tc, x_bytes, x_scale, w0, wr, br, a, b
 
         def soft_recip(step):
             h = int(step[2])
-            nc.vector.reciprocal(out=rs[h][:], in_=ss[h][:])
-
-        def soft_norm(step):
-            h = int(step[2])
-            for j in range(2):
-                nc.gpsimd.tensor_scalar(
-                    out=gn[h][:, j, :], in0=ex[h][:, j, :], scalar1=rs[h][:, j : j + 1], scalar2=float(E), op0=ALU.mult, op1=ALU.mult
-                )
-
-        def soft_turn(step):
-            h = int(step[2])
-            banks[step] = bank("tr", 2, [P, 2, P])
-            for j in range(2):
-                nc.tensor.transpose(banks[step][:, j, :], gn[h][:, j, :], ident[:])
-
-        def soft_out(step):
-            h = int(step[2])
-            copy(step, gT[:, 256 * h : 256 * h + 256], banks["sT%d" % h][:].rearrange("p j n -> p (j n)"))
+            nc.vector.tensor_scalar(out=sd[h][:], in0=ss[h][:], scalar1=1.0 / E, scalar2=None, op0=ALU.mult)
+            nc.vector.reciprocal(out=rs[h][:], in_=sd[h][:])
 
         def zmul(step):
             i = int(step[1])
-            nc.vector.tensor_tensor(
-                out=zg[:, i, :].rearrange("p (n t) -> p n t", t=4),
-                in0=banks["u%d" % i][:].rearrange("p t n -> p n t"),
-                in1=gT[:, P * i : P * i + P].unsqueeze(2).to_broadcast([P, P, 4]),
-                op=ALU.mult,
+            h, j = i // 2, i % 2
+            nc.vector.scalar_tensor_tensor(
+                out=zb[:, i, :].rearrange("p (e c) -> p e c", c=4),
+                in0=banks["u%d" % i][:].rearrange("p (e c) -> p e c", c=4),
+                scalar=rs[h][:, j : j + 1],
+                in1=ex[h][:, j, :].unsqueeze(2).to_broadcast([P, E, 4]),
+                op0=ALU.mult,
+                op1=ALU.mult,
+            )
+
+        def zturn(step):
+            h = int(step[1])
+            banks[step] = bank("tr", 2, [P, 4, P])
+            for j in range(2):
+                words = zb[:, 2 * h + j, :].bitcast(F32)
+                for u in range(2):
+                    nc.tensor.transpose(banks[step][:, 2 * j + u, :], words[:, u:256:2], ident[:])
+
+        def zturn_out(step):
+            h = int(step[1])
+            copy(
+                step,
+                zg[:, 2 * h : 2 * h + 2, :].rearrange("p i n -> p (i n)").bitcast(F32).rearrange("p (i r u) -> p i r u", i=2, u=2),
+                banks["Y%d" % h][:].rearrange("p (i u) r -> p i r u", u=2),
             )
 
         def zquant(step):
@@ -308,9 +308,11 @@ def tile_rankwisemoloradenserouter_kernel(tc, x_bytes, x_scale, w0, wr, br, a, b
             "sM": soft_min,
             "sE": soft_exp,
             "sR": soft_recip,
-            "sN": soft_norm,
-            "sT": soft_turn,
-            "sC": soft_out,
+            "Y": zturn,
+            "H": zturn_out,
+            "bv": bias_cast,
+            "bt": bias_spread,
+            "bs": bias_out,
             "z": zmul,
             "k": zquant,
             "o": base,
@@ -323,7 +325,7 @@ def tile_rankwisemoloradenserouter_kernel(tc, x_bytes, x_scale, w0, wr, br, a, b
         nc.vector.memset(warm[:], 0.0)
         with tc.manual_schedule():
             nc.scalar.activation(out=warm[:], in_=warm[:], func=ACT.Exp)
-            for key in "v x01 br a1 w1 x23 x47 a0 w0 wr b".split():
+            for key in "v wr br x01 a1 x23 a0 x47 b w1 w0".split():
                 load(key)
             for step in ORDER:
                 fn = steps.get(step[:2])

@@ -177,7 +177,7 @@ def tile_rankwisemoloradenserouter_kernel(tc, x_bytes, x_scale, w0, wr, br, a, b
             else:
                 src = raw[key][:, :, P * h : P * h + P]
             dst = grp[key][:, 512 * h : 512 * h + 512]
-            copy(step, dst.rearrange("p (c j) -> p c j", j=4), src.rearrange("p j c -> p c j"))
+            copy(step, dst.rearrange("p (c i j) -> p c j i", i=4, j=4), src.rearrange("p j (c i) -> p c j i", i=4))
 
         def wquant(step):
             k = step[1:]

@@ -5,6 +5,11 @@ from concourse.masks import make_identity
 
 T, D, F, E, R = 1024, 1024, 1024, 128, 512
 P = 128
+PACK = 4
+PASSES = D // (P * PACK)
+TILES = T // P
+HALF = 512
+QUARTER = 128
 FLOPS = 2 * T * (D * (F + E + R) + R * F)
 
 F32 = mybir.dt.float32
@@ -14,27 +19,24 @@ U8 = mybir.dt.uint8
 FP8 = mybir.dt.float8_e4m3fn
 FP8X4 = mybir.dt.float8_e4m3fn_x4
 ALU = mybir.AluOpType
-ACT = mybir.ActivationFunctionType
+EXP = mybir.ActivationFunctionType.Exp
+FREE = mybir.AxisListType.X
+
+FIRST_TILE = 1
+LAST_OUT = (7, 0)
+LOADS = "scale wr bias x01 a0 x23 a1 x47 w0 w1 b"
 
 ORDER = """
-Bc Iwr.0 Iwr.1 Sc0 Sc1 Qwr W0 bv Ia1.0 W1 X0 Ia1.2 Ia1.1 W3
-X1 bt C0 Ia1.3 W2 X3 C1 bs q0 Ia0.1 X2 q1 W5 l0
-Ia0.0 l1 C3 W4 C2 X5 Ia0.2 sA0 X4 Ib0.1 Qa1 Ia0.3 sM0 q3
-C5 Qa0 l3 C4 q2 u0 q5 sE0 q4 l2 Iw11.0 l5 sR0 l4
-W6 u3 Ib0.0 Iw10.3 sA1 X6 Iw10.1 Ib0.2 z0 Ib0.3 Iw00.0 u1 Iw10.2 W7
-Iw10.0 sM1 Iw00.2 X7 z1 Iw00.3 Iw00.1 Qw10 C6 sA2 sE1 Y0 Qw00 Ib1.3
-u2 sR1 H0 sM2 o0.0 q6 Iw11.3 o3.0 z2 sE2 o1.0 z3 C7 u4
-sR2 k0 Ib1.2 Y1 Qb0 Iw11.2 u5 z4 Iw01.2 p0.0 q7 u6 Iw11.1 H1
-l6 z5 p1.0 e0.0 l7 Ib1.0 Iw01.0 k1 o2.0 D0.0  Iw01.3 Y2 Iw01.1 Qw11
-p2.0 e1.0 Qw01 u7 Ib1.1 D1.0 p3.0 o2.1 e2.0 Qb1 H2 o1.1 D2.0 e3.0
-p2.1 sA3 o4.0 D3.0 k2 e2.1 p1.1 sM3 p4.0 o5.1 e1.1 sE3 e4.0 p5.1
-sR3 o5.0 e5.1 z7 D4.0 o4.1 z6 D1.1 p5.0 p4.1 o0.1 e5.0 D5.1 Y3
-e4.1 D5.0 p0.1 D2.1 H3 o3.1 D4.1 e0.1 o6.0 k3 p3.1 D0.1 o7.0 e3.1
-p6.0 p7.0 D3.1 o7.1 e6.0 e7.0 p7.1 D6.0 o6.1 e7.1 p6.1 D7.0 e6.1 D7.1
-D6.1
-""".split()
-FIRST_W = [s for s in ORDER if s[0] == "W"][0]
-ON_V = set("Iwr.1 Sc0 Iw10.1 Iw00.0 Iw00.1 Iw11.1 Ib1.0 Iw01.3 e3.0 e1.1 e7.0 e7.1".split())
+Iwr.1 Iwr.0* F0* F1 Kwr W1 Ia0.1 W0 Ia0.2 T1 Ia0.3 W3 T0 N Ia0.0 C1 W2 Ia1.0 T3 C0
+G W4 Ia1.3 T2 C3 Q0 Ia1.1 T4 Q1 W5 Ia1.2 L0 L1 C2 W7 C4 T5 Iw00.3 Q4 T7
+Iw00.2 Q2 A0 Iw00.0 L2 Ka1 L4 C5 Ka0 Iw00.1 Q3 U1 Iw10.0 Q5 M0 U0 Iw01.0 W6 L3 L5
+Iw10.2 E0 A2 T6 Iw10.3 R0 A1 Ib0.2 M2 Z1 Iw10.1 Z0 E2 U4 C7 R2 U5 M1 Ib0.1 Z4
+Y0 E1 Z5 U3 Ib0.0 Kw00 U2 C6 Kw10 Ib0.3 Y2 Q7 Iw11.3 O1.0 R1 Q6 H0 Kb0 O4.0 Iw11.2
+L6 V0 O0.0 Iw01.3 Z2 L7 P0.0 H2 Z3 P1.0 U6 Ib1.3 D0.0* Y1 D1.0 V2 Iw01.2* O5.0 Iw01.1 Ib1.0*
+Ib1.2* P4.0 H1 O3.0 Iw11.0* D4.0 Iw11.1* P5.0 V1 U7 Ib1.1 Kw01 P3.0 D5.0 O2.0 Kw11 D3.0 P2.0 A3 O2.1
+Kb1 D2.0 O1.1 M3 P2.1 E3 P1.1 O5.1 D2.1 R3 P5.1 D1.1 O0.1 Z6 D5.1 O4.1 Z7 P0.1 P4.1 Y3
+D0.1* D4.1 O3.1 H3* O7.1 V3 P3.1 O6.0 D3.1 P7.1 P6.0 O6.1 D7.1 D6.0* P6.1 O7.0 D6.1 P7.0 D7.0
+"""
 
 
 def tile_rankwisemoloradenserouter_kernel(tc, x_bytes, x_scale, w0, wr, br, a, b, out):
@@ -43,292 +45,280 @@ def tile_rankwisemoloradenserouter_kernel(tc, x_bytes, x_scale, w0, wr, br, a, b
         keep = ctx.enter_context(tc.tile_pool(name="keep", bufs=1))
         psum = ctx.enter_context(tc.psum_pool(name="psum", bufs=1))
 
-        def sb(name, shape, dtype):
+        def sbuf(name, shape, dtype):
             return keep.tile(shape, dtype, name=name, tag=name, align_bytes=64)
 
-        def bank(tag, bufs, shape):
-            return psum.tile(shape, F32, name=tag, tag=tag, bufs=bufs)
+        bank_counts = {"turn": 2, "logit": 1, "u": 2, "out": 3}
 
-        ident = sb("ident", [P, P], F32)
-        warm = sb("warm", [P, 1], F32)
-        scol = sb("scol", [P, 2, 4], F32)
-        srow = sb("srow", [P, 2, P, 4], F32)
-        xr = sb("xr", [P, 8, D], U8)
-        xb = sb("xb", [P, 8, D], BF16)
-        xg = sb("xg", [P, 8, 4 * 2 * P], BF16)
-        xc = sb("xc", [P, 8, 2 * P], U32)
-        xs = sb("xs", [P, 8, 2 * P], U8)
-        brc = sb("brc", [P, 1], BF16)
-        brf = sb("brf", [P, 1], F32)
-        brb = sb("brb", [P, E], F32)
-        zb = sb("zb", [P, 8, R], BF16)
-        zg = sb("zg", [P, 8, P * 4], BF16)
-        zc = sb("zc", [P, 8, P], U32)
-        zs = sb("zs", [P, 8, P], U8)
-        osb = sb("osb", [P, 8, F], F32)
-        raw, grp, cod, scl = {}, {}, {}, {}
-        rawb = sb("raw_b", [P, 4, F], BF16)
-        raww = [sb("raw_w%d" % g, [P, 4, F], BF16) for g in range(2)]
-        for k in ("a0", "a1", "b0", "b1", "w00", "w10", "w01", "w11"):
-            if k[0] == "a":
-                raw[k] = sb("raw_" + k, [P, 4, 512], BF16)
-            else:
-                n = int(k[-1])
-                raw[k] = (rawb if k[0] == "b" else raww[int(k[1])])[:, :, 512 * n : 512 * n + 512]
-            grp[k] = sb("grp_" + k, [P, 512 * 4], BF16)
-            cod[k] = sb("cod_" + k, [P, 512], U32)
-            scl[k] = sb("scl_" + k, [P, 512], U8)
-        raw["wr"] = sb("raw_wr", [P, 2, 4, E], BF16)
-        grp["wr"] = sb("grp_wr", [P, 2 * E * 4], BF16)
-        cod["wr"] = sb("cod_wr", [P, 2 * E], U32)
-        scl["wr"] = sb("scl_wr", [P, 2 * E], U8)
-        nl = [sb("nl%d" % h, [P, 2, E], F32) for h in range(4)]
-        nm = [sb("nm%d" % h, [P, 2], F32) for h in range(4)]
-        ss = [sb("ss%d" % h, [P, 2], F32) for h in range(4)]
-        rs = [sb("rs%d" % h, [P, 2], F32) for h in range(4)]
-        ex = [sb("ex%d" % h, [P, 2, E], F32) for h in range(4)]
-        sd = [sb("sd%d" % h, [P, 2], F32) for h in range(4)]
+        def bank(tag, shape):
+            return psum.tile(shape, F32, name=tag, tag=tag, bufs=bank_counts[tag])
 
-        x_v = x_bytes.rearrange("(p i) k -> p i k", i=8)
-        out_v = out.rearrange("(p i) f -> p i f", i=8)
-        wr_v = wr.rearrange("(g p j) e -> p g j e", p=P, j=4)
-        a_v = a.rearrange("(g p j) r -> g p j r", p=P, j=4)
-        w0_v = w0.rearrange("(g p j) f -> g p j f", p=P, j=4)
-        b_v = b.rearrange("(p j) f -> p j f", j=4)
+        ident = sbuf("ident", [P, P], F32)
+        warm = sbuf("warm", [P, 1], F32)
+        scale_col = sbuf("scale_col", [P, PASSES, PACK], F32)
+        scale_row = sbuf("scale_row", [P, PASSES, P, PACK], F32)
+        bias_raw = sbuf("bias_raw", [P, 1], BF16)
+        bias_col = sbuf("bias_col", [P, 1], F32)
+        bias_row = sbuf("bias_row", [P, E], F32)
+        x_raw = sbuf("x_raw", [P, TILES, D], U8)
+        x_wide = sbuf("x_wide", [P, TILES, D], BF16)
+        x_turned = sbuf("x_turned", [P, TILES, PASSES * P * PACK], BF16)
+        x_codes = sbuf("x_codes", [P, TILES, PASSES * P], U32)
+        x_scales = sbuf("x_scales", [P, TILES, PASSES * P], U8)
+        z_wide = sbuf("z_wide", [P, TILES, R], BF16)
+        z_turned = sbuf("z_turned", [P, TILES, P * PACK], BF16)
+        z_codes = sbuf("z_codes", [P, TILES, P], U32)
+        z_scales = sbuf("z_scales", [P, TILES, P], U8)
+        result = sbuf("result", [P, TILES, F], F32)
+        pair = {}
+        for h in range(TILES // 2):
+            pair["logits", h] = sbuf("logits%d" % h, [P, 2, E], F32)
+            pair["min", h] = sbuf("min%d" % h, [P, 2], F32)
+            pair["exp", h] = sbuf("exp%d" % h, [P, 2, E], F32)
+            pair["sum", h] = sbuf("sum%d" % h, [P, 2], F32)
+            pair["mean", h] = sbuf("mean%d" % h, [P, 2], F32)
+            pair["recip", h] = sbuf("recip%d" % h, [P, 2], F32)
+
+        wr_raw = sbuf("wr_raw", [P, PASSES, PACK, E], BF16)
+        a_raw = [sbuf("a_raw%d" % g, [P, PACK, R], BF16) for g in range(PASSES)]
+        w0_raw = [sbuf("w0_raw%d" % g, [P, PACK, F], BF16) for g in range(PASSES)]
+        b_raw = sbuf("b_raw", [P, PACK, F], BF16)
+        quarters = {"wr": [wr_raw[:, g] for g in range(PASSES)]}
+
+        def cut(raw, first):
+            return [raw[:, :, first + q * QUARTER : first + (q + 1) * QUARTER] for q in range(HALF // QUARTER)]
+
+        for g in range(PASSES):
+            quarters["a%d" % g] = cut(a_raw[g], 0)
+            for n in range(F // HALF):
+                quarters["w%d%d" % (g, n)] = cut(w0_raw[g], n * HALF)
+        for n in range(F // HALF):
+            quarters["b%d" % n] = cut(b_raw, n * HALF)
+        grouped, codes, scales = {}, {}, {}
+        for w in quarters:
+            columns = len(quarters[w]) * QUARTER
+            grouped[w] = sbuf("grouped_" + w, [P, columns * PACK], BF16)
+            codes[w] = sbuf("codes_" + w, [P, columns], U32)
+            scales[w] = sbuf("scales_" + w, [P, columns], U8)
+
+        x_rows = x_bytes.rearrange("(p i) k -> p i k", i=TILES)
+        out_rows = out.rearrange("(p i) f -> p i f", i=TILES)
+        a_rows = a.rearrange("(g p j) r -> g p j r", p=P, j=PACK)
+        w0_rows = w0.rearrange("(g p j) f -> g p j f", p=P, j=PACK)
+        sources = {
+            "scale": (scale_col[:], x_scale.rearrange("o (g p t) -> p (o g) t", p=P, t=PACK)),
+            "bias": (bias_raw[:], br.rearrange("(p o) -> p o", o=1)),
+            "wr": (wr_raw[:], wr.rearrange("(g p j) e -> p g j e", p=P, j=PACK)),
+            "a0": (a_raw[0][:], a_rows[0]),
+            "a1": (a_raw[1][:], a_rows[1]),
+            "w0": (w0_raw[0][:], w0_rows[0]),
+            "w1": (w0_raw[1][:], w0_rows[1]),
+            "b": (b_raw[:], b.rearrange("(p j) f -> p j f", j=PACK)),
+            "x01": (x_raw[:, 0:2, :], x_rows[:, 0:2, :]),
+            "x23": (x_raw[:, 2:4, :], x_rows[:, 2:4, :]),
+            "x47": (x_raw[:, 4:8, :], x_rows[:, 4:8, :]),
+        }
+
         banks = {}
+        logit_bank = bank("logit", [P, 4, E])
 
-        def load(key):
-            if key == "v":
-                nc.sync.dma_start(out=scol[:], in_=x_scale.rearrange("o (g p t) -> p (o g) t", p=P, t=4))
-            elif key == "br":
-                nc.sync.dma_start(out=brc[:], in_=br.rearrange("(p o) -> p o", o=1))
-            elif key[0] == "x":
-                i0, i1 = int(key[1]), int(key[2]) + 1
-                nc.sync.dma_start(out=xr[:, i0:i1, :], in_=x_v[:, i0:i1, :])
-            elif key == "wr":
-                nc.sync.dma_start(out=raw["wr"][:], in_=wr_v)
-            elif key[0] == "a":
-                nc.sync.dma_start(out=raw[key][:], in_=a_v[int(key[1])])
-            elif key == "b":
-                nc.sync.dma_start(out=rawb[:], in_=b_v)
-            else:
-                nc.sync.dma_start(out=raww[int(key[1])][:], in_=w0_v[int(key[1])])
-
-        def copy(step, out_ap, in_ap):
-            if step in ON_V:
+        def copy(on_vector, out_ap, in_ap):
+            if on_vector:
                 nc.vector.tensor_copy(out=out_ap, in_=in_ap)
             else:
                 nc.scalar.copy(out=out_ap, in_=in_ap)
 
-        def spread(step):
-            for g in range(2):
-                banks["B%d" % g] = bank("tr", 2, [P, 4, P])
-                for t in range(4):
-                    nc.tensor.transpose(banks["B%d" % g][:, t, :], scol[:, g, t : t + 1].to_broadcast([P, P]), ident[:])
-
-        def bias_cast(step):
-            nc.vector.tensor_copy(out=brf[:], in_=brc[:])
-
-        def bias_spread(step):
-            banks["br"] = bank("lg", 1, [P, P])
-            nc.tensor.transpose(banks["br"][:], brf[:].to_broadcast([P, P]), ident[:])
-
-        def bias_out(step):
-            nc.scalar.copy(out=brb[:], in_=banks["br"][:])
-
-        def spread_out(step):
-            g = int(step[2])
-            copy(step, srow[:, g], banks["B%d" % g][:].rearrange("p t n -> p n t"))
-
-        def widen(step):
-            i = int(step[1])
-            halves = 2 if step == FIRST_W else 1
-            w = D // halves
-            flat = srow[:].rearrange("p g n t -> p (g n t)")
-            for h in range(halves):
-                c = slice(h * w, h * w + w)
-                nc.vector.tensor_tensor(out=xb[:, i, c], in0=xr[:, i, c].bitcast(FP8), in1=flat[:, c], op=ALU.mult)
-
-        def turn(step):
-            i = int(step[1])
-            banks[step] = bank("tr", 2, [P, 4, P])
-            words = xb[:, i, :].bitcast(F32)
-            for g in range(2):
-                for u in range(2):
-                    nc.tensor.transpose(banks[step][:, 2 * g + u, :], words[:, 256 * g + u : 256 * (g + 1) : 2], ident[:])
-
-        def turn_out(step):
-            i = int(step[1])
-            copy(
-                step,
-                xg[:, i, :].bitcast(F32).rearrange("p (g r u) -> p g r u", g=2, u=2),
-                banks["X%d" % i][:].rearrange("p (g u) r -> p g r u", u=2),
-            )
-
-        def xquant(step):
-            i = int(step[1])
-            nc.vector.quantize_mx(out=xc[:, i, :].bitcast(FP8X4), scales=xs[:, i, :], in_=xg[:, i, :])
-
-        def inter(step):
-            key, h = step[1:].split(".")
-            h = int(h)
-            if key == "wr":
-                src = raw["wr"][:, h]
-            else:
-                src = raw[key][:, :, P * h : P * h + P]
-            dst = grp[key][:, 512 * h : 512 * h + 512]
-            copy(step, dst.rearrange("p (c i j) -> p c j i", i=4, j=4), src.rearrange("p j (c i) -> p c j i", i=4))
-
-        def wquant(step):
-            k = step[1:]
-            nc.vector.quantize_mx(out=cod[k][:].bitcast(FP8X4), scales=scl[k][:], in_=grp[k][:])
-
-        def mx(out_ap, lc, ls, rc, rsc, start, stop):
+        def mx(out_ap, weights, weight_scales, moving, moving_scales, start, stop):
             nc.tensor.matmul_mx(
-                out=out_ap, lhsT=lc.bitcast(FP8X4), lhsT_scale=ls, rhs=rc.bitcast(FP8X4), rhs_scale=rsc, start=start, stop=stop
+                out=out_ap,
+                lhsT=weights.bitcast(FP8X4),
+                lhsT_scale=weight_scales,
+                rhs=moving.bitcast(FP8X4),
+                rhs_scale=moving_scales,
+                start=start,
+                stop=stop,
             )
 
-        def logits(step):
-            i = int(step[1])
-            if "L%d" % (i // 4) not in banks:
-                banks["L%d" % (i // 4)] = bank("lg", 1, [P, 4, E])
-            for g in range(2):
-                c = slice(P * g, P * g + P)
-                mx(banks["L%d" % (i // 4)][:, i % 4, :], xc[:, i, c], xs[:, i, c], cod["wr"][:, c], scl["wr"][:, c], g == 0, g == 1)
+        def spread(out_ap, column):
+            nc.tensor.transpose(out_ap, column.to_broadcast([P, P]), ident[:])
 
-        def down(step):
-            i = int(step[1])
-            banks[step] = bank("u", 2, [P, R])
-            for g in range(2):
-                c = slice(P * g, P * g + P)
-                k = "a%d" % g
-                mx(banks[step][:], xc[:, i, c], xs[:, i, c], cod[k][:], scl[k][:], g == 0, g == 1)
+        def spread_scales():
+            for g in range(PASSES):
+                banks["F", g] = bank("turn", [P, PACK, P])
+                for t in range(PACK):
+                    spread(banks["F", g][:, t, :], scale_col[:, g, t : t + 1])
 
-        def soft_add(step):
-            h = int(step[2])
+        def fetch_scales(v, g):
+            copy(v, scale_row[:, g], banks["F", g][:].rearrange("p t n -> p n t"))
+
+        def spread_bias(v):
+            spread(logit_bank[:, 0, :], bias_col[:])
+
+        def fetch_bias(v):
+            copy(v, bias_row[:], logit_bank[:, 0, :])
+
+        def widen(v, i):
+            flat = scale_row[:].rearrange("p g n t -> p (g n t)")
+            pieces = PASSES if i == FIRST_TILE else 1
+            for c in range(pieces):
+                k = slice(c * D // pieces, (c + 1) * D // pieces)
+                nc.vector.tensor_tensor(out=x_wide[:, i, k], in0=x_raw[:, i, k].bitcast(FP8), in1=flat[:, k], op=ALU.mult)
+
+        def turn_x(v, i):
+            banks["T", i] = bank("turn", [P, 2 * PASSES, P])
+            words = x_wide[:, i, :].bitcast(F32)
+            for g in range(PASSES):
+                for u in range(2):
+                    pick = slice(2 * P * g + u, 2 * P * (g + 1), 2)
+                    nc.tensor.transpose(banks["T", i][:, 2 * g + u, :], words[:, pick], ident[:])
+
+        def fetch_x(v, i):
+            words = x_turned[:, i, :].bitcast(F32).rearrange("p (g r u) -> p g r u", g=PASSES, u=2)
+            copy(v, words, banks["T", i][:].rearrange("p (g u) r -> p g r u", u=2))
+
+        def quantise_x(v, i):
+            nc.vector.quantize_mx(out=x_codes[:, i, :].bitcast(FP8X4), scales=x_scales[:, i, :], in_=x_turned[:, i, :])
+
+        def interleave(v, w, q):
+            group = grouped[w][:, q * QUARTER * PACK : (q + 1) * QUARTER * PACK]
+            copy(
+                v,
+                group.rearrange("p (c i j) -> p c j i", i=4, j=PACK),
+                quarters[w][q].rearrange("p j (c i) -> p c j i", i=4),
+            )
+
+        def quantise_w(v, w):
+            nc.vector.quantize_mx(out=codes[w][:].bitcast(FP8X4), scales=scales[w][:], in_=grouped[w][:])
+
+        def x_pass(i, g):
+            c = slice(g * P, (g + 1) * P)
+            return x_codes[:, i, c], x_scales[:, i, c]
+
+        def logits(v, i):
+            for g in range(PASSES):
+                c = slice(g * E, (g + 1) * E)
+                rhs = codes["wr"][:, c], scales["wr"][:, c]
+                mx(logit_bank[:, i % 4, :], *x_pass(i, g), *rhs, g == 0, g == PASSES - 1)
+
+        def bias_logits(v, h):
+            j = 2 * (h % 2)
             nc.vector.scalar_tensor_tensor(
-                out=nl[h][:],
-                in0=banks["L%d" % (h // 2)][:, 2 * (h % 2) : 2 * (h % 2) + 2, :],
+                out=pair["logits", h][:],
+                in0=logit_bank[:, j : j + 2, :],
                 scalar=-1.0,
-                in1=brb[:].unsqueeze(1).to_broadcast([P, 2, E]),
+                in1=bias_row[:].unsqueeze(1).to_broadcast([P, 2, E]),
                 op0=ALU.mult,
                 op1=ALU.subtract,
             )
 
-        def soft_min(step):
-            h = int(step[2])
-            nc.vector.tensor_reduce(out=nm[h][:], in_=nl[h][:], axis=mybir.AxisListType.X, op=ALU.min)
+        def min_logits(v, h):
+            nc.vector.tensor_reduce(out=pair["min", h][:], in_=pair["logits", h][:], axis=FREE, op=ALU.min)
 
-        def soft_exp(step):
-            h = int(step[2])
+        def exp_logits(v, h):
             for j in range(2):
                 nc.scalar.activation(
-                    out=ex[h][:, j, :],
-                    in_=nl[h][:, j, :],
-                    func=ACT.Exp,
-                    bias=nm[h][:, j : j + 1],
+                    out=pair["exp", h][:, j, :],
+                    in_=pair["logits", h][:, j, :],
+                    func=EXP,
+                    bias=pair["min", h][:, j : j + 1],
                     scale=-1.0,
-                    accum_out=ss[h][:, j : j + 1],
+                    accum_out=pair["sum", h][:, j : j + 1],
                 )
 
-        def soft_recip(step):
-            h = int(step[2])
-            nc.vector.tensor_scalar(out=sd[h][:], in0=ss[h][:], scalar1=1.0 / E, scalar2=None, op0=ALU.mult)
-            nc.vector.reciprocal(out=rs[h][:], in_=sd[h][:])
+        def recip(v, h):
+            nc.vector.tensor_scalar(
+                out=pair["mean", h][:], in0=pair["sum", h][:], scalar1=1.0 / E, scalar2=None, op0=ALU.mult
+            )
+            nc.vector.reciprocal(out=pair["recip", h][:], in_=pair["mean", h][:])
 
-        def zmul(step):
-            i = int(step[1])
+        def down(v, i):
+            banks["U", i] = bank("u", [P, R])
+            for g in range(PASSES):
+                w = "a%d" % g
+                mx(banks["U", i][:], *x_pass(i, g), codes[w][:], scales[w][:], g == 0, g == PASSES - 1)
+
+        def scale_u(v, i):
             h, j = i // 2, i % 2
             nc.vector.scalar_tensor_tensor(
-                out=zb[:, i, :].rearrange("p (e c) -> p e c", c=4),
-                in0=banks["u%d" % i][:].rearrange("p (e c) -> p e c", c=4),
-                scalar=rs[h][:, j : j + 1],
-                in1=ex[h][:, j, :].unsqueeze(2).to_broadcast([P, E, 4]),
+                out=z_wide[:, i, :].rearrange("p (e c) -> p e c", c=R // E),
+                in0=banks["U", i][:].rearrange("p (e c) -> p e c", c=R // E),
+                scalar=pair["recip", h][:, j : j + 1],
+                in1=pair["exp", h][:, j, :].unsqueeze(2).to_broadcast([P, E, R // E]),
                 op0=ALU.mult,
                 op1=ALU.mult,
             )
 
-        def zturn(step):
-            h = int(step[1])
-            banks[step] = bank("tr", 2, [P, 4, P])
+        def turn_z(v, h):
+            banks["Y", h] = bank("turn", [P, 4, P])
             for j in range(2):
-                words = zb[:, 2 * h + j, :].bitcast(F32)
+                words = z_wide[:, 2 * h + j, :].bitcast(F32)
                 for u in range(2):
-                    nc.tensor.transpose(banks[step][:, 2 * j + u, :], words[:, u:256:2], ident[:])
+                    nc.tensor.transpose(banks["Y", h][:, 2 * j + u, :], words[:, u : 2 * P : 2], ident[:])
 
-        def zturn_out(step):
-            h = int(step[1])
-            copy(
-                step,
-                zg[:, 2 * h : 2 * h + 2, :].rearrange("p i n -> p (i n)").bitcast(F32).rearrange("p (i r u) -> p i r u", i=2, u=2),
-                banks["Y%d" % h][:].rearrange("p (i u) r -> p i r u", u=2),
-            )
+        def both(tensor, h):
+            return tensor[:, 2 * h : 2 * h + 2, :].rearrange("p i n -> p (i n)")
 
-        def zquant(step):
-            c = slice(2 * int(step[1]), 2 * int(step[1]) + 2)
-            nc.vector.quantize_mx(
-                out=zc[:, c, :].rearrange("p i n -> p (i n)").bitcast(FP8X4),
-                scales=zs[:, c, :].rearrange("p i n -> p (i n)"),
-                in_=zg[:, c, :].rearrange("p i n -> p (i n)"),
-            )
+        def fetch_z(v, h):
+            words = both(z_turned, h).bitcast(F32).rearrange("p (i r u) -> p i r u", i=2, u=2)
+            copy(v, words, banks["Y", h][:].rearrange("p (i u) r -> p i r u", u=2))
 
-        def base(step):
-            i, n = int(step[1]), step[3]
-            banks[step[1:]] = bank("o", 3, [P, 512])
-            for g in range(2):
-                c = slice(P * g, P * g + P)
-                k = "w%d%s" % (g, n)
-                mx(banks[step[1:]][:], xc[:, i, c], xs[:, i, c], cod[k][:], scl[k][:], g == 0, False)
+        def quantise_z(v, h):
+            nc.vector.quantize_mx(out=both(z_codes, h).bitcast(FP8X4), scales=both(z_scales, h), in_=both(z_turned, h))
 
-        def up(step):
-            i, n = int(step[1]), step[3]
-            k = "b" + n
-            mx(banks[step[1:]][:], zc[:, i, :], zs[:, i, :], cod[k][:], scl[k][:], False, True)
+        def base(v, i, n):
+            banks["O", i, n] = bank("out", [P, HALF])
+            for g in range(PASSES):
+                w = "w%d%d" % (g, n)
+                mx(banks["O", i, n][:], *x_pass(i, g), codes[w][:], scales[w][:], g == 0, False)
 
-        def evac(step):
-            i, n = int(step[1]), int(step[3])
-            copy(step, osb[:, i, 512 * n : 512 * n + 512], banks[step[1:]][:])
+        def up(v, i, n):
+            w = "b%d" % n
+            mx(banks["O", i, n][:], z_codes[:, i, :], z_scales[:, i, :], codes[w][:], scales[w][:], False, True)
 
-        def store(step):
-            i, n = int(step[1]), int(step[3])
-            nc.sync.dma_start(out=out_v[:, i, 512 * n : 512 * n + 512], in_=osb[:, i, 512 * n : 512 * n + 512])
+        def deliver(v, i, n):
+            pieces = 2 if (i, n) == LAST_OUT else 1
+            width = HALF // pieces
+            for s in range(pieces):
+                c = slice(n * HALF + s * width, n * HALF + (s + 1) * width)
+                copy(v, result[:, i, c], banks["O", i, n][:, s * width : (s + 1) * width])
+                nc.sync.dma_start(out=out_rows[:, i, c], in_=result[:, i, c])
 
-        steps = {
-            "Bc": spread,
-            "Sc": spread_out,
+        functions = {
+            "F": fetch_scales,
+            "N": spread_bias,
+            "G": fetch_bias,
             "W": widen,
-            "X": turn,
-            "C": turn_out,
-            "q": xquant,
-            "I": inter,
-            "Q": wquant,
-            "l": logits,
-            "u": down,
-            "sA": soft_add,
-            "sM": soft_min,
-            "sE": soft_exp,
-            "sR": soft_recip,
-            "Y": zturn,
-            "H": zturn_out,
-            "bv": bias_cast,
-            "bt": bias_spread,
-            "bs": bias_out,
-            "z": zmul,
-            "k": zquant,
-            "o": base,
-            "p": up,
-            "e": evac,
-            "D": store,
+            "T": turn_x,
+            "C": fetch_x,
+            "Q": quantise_x,
+            "I": interleave,
+            "K": quantise_w,
+            "L": logits,
+            "A": bias_logits,
+            "M": min_logits,
+            "E": exp_logits,
+            "R": recip,
+            "U": down,
+            "Z": scale_u,
+            "Y": turn_z,
+            "H": fetch_z,
+            "V": quantise_z,
+            "O": base,
+            "P": up,
+            "D": deliver,
         }
 
-        make_identity(nc, ident[:])
         nc.vector.memset(warm[:], 0.0)
+        nc.scalar.activation(out=warm[:], in_=warm[:], func=EXP)
+        make_identity(nc, ident[:])
         with tc.manual_schedule():
-            nc.scalar.activation(out=warm[:], in_=warm[:], func=ACT.Exp)
-            for key in "v wr br x01 a1 x23 a0 x47 b w1 w0".split():
-                load(key)
-            for step in ORDER:
-                fn = steps.get(step[:2])
-                if fn is None:
-                    fn = steps[step[0]]
-                fn(step)
+            for key in LOADS.split():
+                tile_ap, hbm_ap = sources[key]
+                nc.sync.dma_start(out=tile_ap, in_=hbm_ap)
+            nc.gpsimd.tensor_copy(out=bias_col[:], in_=bias_raw[:])
+            spread_scales()
+            for step in ORDER.split():
+                on_vector = step[-1] == "*"
+                fields = step[1:].replace("*", "").split(".")
+                args = [int(s) if s in "0123456789" else s for s in fields if s]
+                functions[step[0]](on_vector, *args)

from contextlib import ExitStack

import concourse.mybir as mybir
from concourse.masks import make_identity

T, D, F, E, R = 1024, 1024, 1024, 128, 512
P = 128
PACK = 4
PASSES = D // (P * PACK)
TILES = T // P
HALF = 512
QUARTER = 128
FLOPS = 2 * T * (D * (F + E + R) + R * F)

F32 = mybir.dt.float32
BF16 = mybir.dt.bfloat16
U32 = mybir.dt.uint32
U8 = mybir.dt.uint8
FP8 = mybir.dt.float8_e4m3fn
FP8X4 = mybir.dt.float8_e4m3fn_x4
ALU = mybir.AluOpType
EXP = mybir.ActivationFunctionType.Exp
FREE = mybir.AxisListType.X

FIRST_TILE = 1
LAST_OUT = (7, 0)
LOADS = "scale wr bias x01 a0 x23 a1 x47 w0 w1 b"

ORDER = """
Iwr.1 Iwr.0* F0* F1 Kwr W1 Ia0.1 W0 Ia0.2 T1 Ia0.3 W3 T0 N Ia0.0 C1 W2 Ia1.0 T3 C0
G W4 Ia1.3 T2 C3 Q0 Ia1.1 T4 Q1 W5 Ia1.2 L0 L1 C2 W7 C4 T5 Iw00.3 Q4 T7
Iw00.2 Q2 A0 Iw00.0 L2 Ka1 L4 C5 Ka0 Iw00.1 Q3 U1 Iw10.0 Q5 M0 U0 Iw01.0 W6 L3 L5
Iw10.2 E0 A2 T6 Iw10.3 R0 A1 Ib0.2 M2 Z1 Iw10.1 Z0 E2 U4 C7 R2 U5 M1 Ib0.1 Z4
Y0 E1 Z5 U3 Ib0.0 Kw00 U2 C6 Kw10 Ib0.3 Y2 Q7 Iw11.3 O1.0 R1 Q6 H0 Kb0 O4.0 Iw11.2
L6 V0 O0.0 Iw01.3 Z2 L7 P0.0 H2 Z3 P1.0 U6 Ib1.3 D0.0* Y1 D1.0 V2 Iw01.2* O5.0 Iw01.1 Ib1.0*
Ib1.2* P4.0 H1 O3.0 Iw11.0* D4.0 Iw11.1* P5.0 V1 U7 Ib1.1 Kw01 P3.0 D5.0 O2.0 Kw11 D3.0 P2.0 A3 O2.1
Kb1 D2.0 O1.1 M3 P2.1 E3 P1.1 O5.1 D2.1 R3 P5.1 D1.1 O0.1 Z6 D5.1 O4.1 Z7 P0.1 P4.1 Y3
D0.1* D4.1 O3.1 H3* O7.1 V3 P3.1 O6.0 D3.1 P7.1 P6.0 O6.1 D7.1 D6.0* P6.1 O7.0 D6.1 P7.0 D7.0
"""


def tile_rankwisemoloradenserouter_kernel(tc, x_bytes, x_scale, w0, wr, br, a, b, out):
    nc = tc.nc
    with ExitStack() as ctx:
        keep = ctx.enter_context(tc.tile_pool(name="keep", bufs=1))
        psum = ctx.enter_context(tc.psum_pool(name="psum", bufs=1))

        def sbuf(name, shape, dtype):
            return keep.tile(shape, dtype, name=name, tag=name, align_bytes=64)

        bank_counts = {"turn": 2, "logit": 1, "u": 2, "out": 3}

        def bank(tag, shape):
            return psum.tile(shape, F32, name=tag, tag=tag, bufs=bank_counts[tag])

        ident = sbuf("ident", [P, P], F32)
        warm = sbuf("warm", [P, 1], F32)
        scale_col = sbuf("scale_col", [P, PASSES, PACK], F32)
        scale_row = sbuf("scale_row", [P, PASSES, P, PACK], F32)
        bias_raw = sbuf("bias_raw", [P, 1], BF16)
        bias_col = sbuf("bias_col", [P, 1], F32)
        bias_row = sbuf("bias_row", [P, E], F32)
        x_raw = sbuf("x_raw", [P, TILES, D], U8)
        x_wide = sbuf("x_wide", [P, TILES, D], BF16)
        x_turned = sbuf("x_turned", [P, TILES, PASSES * P * PACK], BF16)
        x_codes = sbuf("x_codes", [P, TILES, PASSES * P], U32)
        x_scales = sbuf("x_scales", [P, TILES, PASSES * P], U8)
        z_wide = sbuf("z_wide", [P, TILES, R], BF16)
        z_turned = sbuf("z_turned", [P, TILES, P * PACK], BF16)
        z_codes = sbuf("z_codes", [P, TILES, P], U32)
        z_scales = sbuf("z_scales", [P, TILES, P], U8)
        result = sbuf("result", [P, TILES, F], F32)
        pair = {}
        for h in range(TILES // 2):
            pair["logits", h] = sbuf("logits%d" % h, [P, 2, E], F32)
            pair["min", h] = sbuf("min%d" % h, [P, 2], F32)
            pair["exp", h] = sbuf("exp%d" % h, [P, 2, E], F32)
            pair["sum", h] = sbuf("sum%d" % h, [P, 2], F32)
            pair["mean", h] = sbuf("mean%d" % h, [P, 2], F32)
            pair["recip", h] = sbuf("recip%d" % h, [P, 2], F32)

        wr_raw = sbuf("wr_raw", [P, PASSES, PACK, E], BF16)
        a_raw = [sbuf("a_raw%d" % g, [P, PACK, R], BF16) for g in range(PASSES)]
        w0_raw = [sbuf("w0_raw%d" % g, [P, PACK, F], BF16) for g in range(PASSES)]
        b_raw = sbuf("b_raw", [P, PACK, F], BF16)
        quarters = {"wr": [wr_raw[:, g] for g in range(PASSES)]}

        def cut(raw, first):
            return [raw[:, :, first + q * QUARTER : first + (q + 1) * QUARTER] for q in range(HALF // QUARTER)]

        for g in range(PASSES):
            quarters["a%d" % g] = cut(a_raw[g], 0)
            for n in range(F // HALF):
                quarters["w%d%d" % (g, n)] = cut(w0_raw[g], n * HALF)
        for n in range(F // HALF):
            quarters["b%d" % n] = cut(b_raw, n * HALF)
        grouped, codes, scales = {}, {}, {}
        for w in quarters:
            columns = len(quarters[w]) * QUARTER
            grouped[w] = sbuf("grouped_" + w, [P, columns * PACK], BF16)
            codes[w] = sbuf("codes_" + w, [P, columns], U32)
            scales[w] = sbuf("scales_" + w, [P, columns], U8)

        x_rows = x_bytes.rearrange("(p i) k -> p i k", i=TILES)
        out_rows = out.rearrange("(p i) f -> p i f", i=TILES)
        a_rows = a.rearrange("(g p j) r -> g p j r", p=P, j=PACK)
        w0_rows = w0.rearrange("(g p j) f -> g p j f", p=P, j=PACK)
        sources = {
            "scale": (scale_col[:], x_scale.rearrange("o (g p t) -> p (o g) t", p=P, t=PACK)),
            "bias": (bias_raw[:], br.rearrange("(p o) -> p o", o=1)),
            "wr": (wr_raw[:], wr.rearrange("(g p j) e -> p g j e", p=P, j=PACK)),
            "a0": (a_raw[0][:], a_rows[0]),
            "a1": (a_raw[1][:], a_rows[1]),
            "w0": (w0_raw[0][:], w0_rows[0]),
            "w1": (w0_raw[1][:], w0_rows[1]),
            "b": (b_raw[:], b.rearrange("(p j) f -> p j f", j=PACK)),
            "x01": (x_raw[:, 0:2, :], x_rows[:, 0:2, :]),
            "x23": (x_raw[:, 2:4, :], x_rows[:, 2:4, :]),
            "x47": (x_raw[:, 4:8, :], x_rows[:, 4:8, :]),
        }

        banks = {}
        logit_bank = bank("logit", [P, 4, E])

        def copy(on_vector, out_ap, in_ap):
            if on_vector:
                nc.vector.tensor_copy(out=out_ap, in_=in_ap)
            else:
                nc.scalar.copy(out=out_ap, in_=in_ap)

        def mx(out_ap, weights, weight_scales, moving, moving_scales, start, stop):
            nc.tensor.matmul_mx(
                out=out_ap,
                lhsT=weights.bitcast(FP8X4),
                lhsT_scale=weight_scales,
                rhs=moving.bitcast(FP8X4),
                rhs_scale=moving_scales,
                start=start,
                stop=stop,
            )

        def spread(out_ap, column):
            nc.tensor.transpose(out_ap, column.to_broadcast([P, P]), ident[:])

        def spread_scales():
            for g in range(PASSES):
                banks["F", g] = bank("turn", [P, PACK, P])
                for t in range(PACK):
                    spread(banks["F", g][:, t, :], scale_col[:, g, t : t + 1])

        def fetch_scales(v, g):
            copy(v, scale_row[:, g], banks["F", g][:].rearrange("p t n -> p n t"))

        def spread_bias(v):
            spread(logit_bank[:, 0, :], bias_col[:])

        def fetch_bias(v):
            copy(v, bias_row[:], logit_bank[:, 0, :])

        def widen(v, i):
            flat = scale_row[:].rearrange("p g n t -> p (g n t)")
            pieces = PASSES if i == FIRST_TILE else 1
            for c in range(pieces):
                k = slice(c * D // pieces, (c + 1) * D // pieces)
                nc.vector.tensor_tensor(out=x_wide[:, i, k], in0=x_raw[:, i, k].bitcast(FP8), in1=flat[:, k], op=ALU.mult)

        def turn_x(v, i):
            banks["T", i] = bank("turn", [P, 2 * PASSES, P])
            words = x_wide[:, i, :].bitcast(F32)
            for g in range(PASSES):
                for u in range(2):
                    pick = slice(2 * P * g + u, 2 * P * (g + 1), 2)
                    nc.tensor.transpose(banks["T", i][:, 2 * g + u, :], words[:, pick], ident[:])

        def fetch_x(v, i):
            words = x_turned[:, i, :].bitcast(F32).rearrange("p (g r u) -> p g r u", g=PASSES, u=2)
            copy(v, words, banks["T", i][:].rearrange("p (g u) r -> p g r u", u=2))

        def quantise_x(v, i):
            nc.vector.quantize_mx(out=x_codes[:, i, :].bitcast(FP8X4), scales=x_scales[:, i, :], in_=x_turned[:, i, :])

        def interleave(v, w, q):
            group = grouped[w][:, q * QUARTER * PACK : (q + 1) * QUARTER * PACK]
            copy(
                v,
                group.rearrange("p (c i j) -> p c j i", i=4, j=PACK),
                quarters[w][q].rearrange("p j (c i) -> p c j i", i=4),
            )

        def quantise_w(v, w):
            nc.vector.quantize_mx(out=codes[w][:].bitcast(FP8X4), scales=scales[w][:], in_=grouped[w][:])

        def x_pass(i, g):
            c = slice(g * P, (g + 1) * P)
            return x_codes[:, i, c], x_scales[:, i, c]

        def logits(v, i):
            for g in range(PASSES):
                c = slice(g * E, (g + 1) * E)
                rhs = codes["wr"][:, c], scales["wr"][:, c]
                mx(logit_bank[:, i % 4, :], *x_pass(i, g), *rhs, g == 0, g == PASSES - 1)

        def bias_logits(v, h):
            j = 2 * (h % 2)
            nc.vector.scalar_tensor_tensor(
                out=pair["logits", h][:],
                in0=logit_bank[:, j : j + 2, :],
                scalar=-1.0,
                in1=bias_row[:].unsqueeze(1).to_broadcast([P, 2, E]),
                op0=ALU.mult,
                op1=ALU.subtract,
            )

        def min_logits(v, h):
            nc.vector.tensor_reduce(out=pair["min", h][:], in_=pair["logits", h][:], axis=FREE, op=ALU.min)

        def exp_logits(v, h):
            for j in range(2):
                nc.scalar.activation(
                    out=pair["exp", h][:, j, :],
                    in_=pair["logits", h][:, j, :],
                    func=EXP,
                    bias=pair["min", h][:, j : j + 1],
                    scale=-1.0,
                    accum_out=pair["sum", h][:, j : j + 1],
                )

        def recip(v, h):
            nc.vector.tensor_scalar(
                out=pair["mean", h][:], in0=pair["sum", h][:], scalar1=1.0 / E, scalar2=None, op0=ALU.mult
            )
            nc.vector.reciprocal(out=pair["recip", h][:], in_=pair["mean", h][:])

        def down(v, i):
            banks["U", i] = bank("u", [P, R])
            for g in range(PASSES):
                w = "a%d" % g
                mx(banks["U", i][:], *x_pass(i, g), codes[w][:], scales[w][:], g == 0, g == PASSES - 1)

        def scale_u(v, i):
            h, j = i // 2, i % 2
            nc.vector.scalar_tensor_tensor(
                out=z_wide[:, i, :].rearrange("p (e c) -> p e c", c=R // E),
                in0=banks["U", i][:].rearrange("p (e c) -> p e c", c=R // E),
                scalar=pair["recip", h][:, j : j + 1],
                in1=pair["exp", h][:, j, :].unsqueeze(2).to_broadcast([P, E, R // E]),
                op0=ALU.mult,
                op1=ALU.mult,
            )

        def turn_z(v, h):
            banks["Y", h] = bank("turn", [P, 4, P])
            for j in range(2):
                words = z_wide[:, 2 * h + j, :].bitcast(F32)
                for u in range(2):
                    nc.tensor.transpose(banks["Y", h][:, 2 * j + u, :], words[:, u : 2 * P : 2], ident[:])

        def both(tensor, h):
            return tensor[:, 2 * h : 2 * h + 2, :].rearrange("p i n -> p (i n)")

        def fetch_z(v, h):
            words = both(z_turned, h).bitcast(F32).rearrange("p (i r u) -> p i r u", i=2, u=2)
            copy(v, words, banks["Y", h][:].rearrange("p (i u) r -> p i r u", u=2))

        def quantise_z(v, h):
            nc.vector.quantize_mx(out=both(z_codes, h).bitcast(FP8X4), scales=both(z_scales, h), in_=both(z_turned, h))

        def base(v, i, n):
            banks["O", i, n] = bank("out", [P, HALF])
            for g in range(PASSES):
                w = "w%d%d" % (g, n)
                mx(banks["O", i, n][:], *x_pass(i, g), codes[w][:], scales[w][:], g == 0, False)

        def up(v, i, n):
            w = "b%d" % n
            mx(banks["O", i, n][:], z_codes[:, i, :], z_scales[:, i, :], codes[w][:], scales[w][:], False, True)

        def deliver(v, i, n):
            pieces = 2 if (i, n) == LAST_OUT else 1
            width = HALF // pieces
            for s in range(pieces):
                c = slice(n * HALF + s * width, n * HALF + (s + 1) * width)
                copy(v, result[:, i, c], banks["O", i, n][:, s * width : (s + 1) * width])
                nc.sync.dma_start(out=out_rows[:, i, c], in_=result[:, i, c])

        functions = {
            "F": fetch_scales,
            "N": spread_bias,
            "G": fetch_bias,
            "W": widen,
            "T": turn_x,
            "C": fetch_x,
            "Q": quantise_x,
            "I": interleave,
            "K": quantise_w,
            "L": logits,
            "A": bias_logits,
            "M": min_logits,
            "E": exp_logits,
            "R": recip,
            "U": down,
            "Z": scale_u,
            "Y": turn_z,
            "H": fetch_z,
            "V": quantise_z,
            "O": base,
            "P": up,
            "D": deliver,
        }

        nc.vector.memset(warm[:], 0.0)
        nc.scalar.activation(out=warm[:], in_=warm[:], func=EXP)
        make_identity(nc, ident[:])
        with tc.manual_schedule():
            for key in LOADS.split():
                tile_ap, hbm_ap = sources[key]
                nc.sync.dma_start(out=tile_ap, in_=hbm_ap)
            nc.gpsimd.tensor_copy(out=bias_col[:], in_=bias_raw[:])
            spread_scales()
            for step in ORDER.split():
                on_vector = step[-1] == "*"
                fields = step[1:].replace("*", "").split(".")
                args = [int(s) if s in "0123456789" else s for s in fields if s]
                functions[step[0]](on_vector, *args)
